import numpy as np
import ml_dtypes


def mxq(x, axis, fmt="e4m3"):
    dtype, down = {"e4m3": (ml_dtypes.float8_e4m3fn, 7), "e5m2": (ml_dtypes.float8_e5m2, 14)}[fmt]
    v = np.moveaxis(np.asarray(x, np.float32).astype(ml_dtypes.bfloat16).astype(np.float64), axis, -1)
    blocks = v.reshape(v.shape[:-1] + (-1, 32))
    amax = np.abs(blocks).max(-1, keepdims=True)
    byte = np.maximum(np.where(amax > 0, np.frexp(amax)[1] - 1 + 127, 0) - down, 1)
    scale = np.exp2(byte - 127.0)
    codes = (blocks / scale).astype(np.float32).astype(dtype).astype(np.float64)
    return np.moveaxis((codes * scale).reshape(v.shape), -1, axis)


WIDE = False


def mx_kscale(k):
    if not WIDE:
        return np.ones(k)
    levels = np.array([30, -30])
    if k % 512:
        return np.exp2(np.random.permutation(np.resize(levels, k // 32))).repeat(32)
    a = np.empty((k // 512, 16))
    for p in range(k // 512):
        a[p, :8] = np.random.permutation(np.resize(levels, 8))
        for g in range(8):
            far = levels[np.abs(levels - a[p, g]) >= 10]
            a[p, g + 8] = far[np.random.randint(len(far))]
    return np.exp2(a.ravel()).repeat(32)


def f64(x):
    return np.asarray(x).astype(np.float64)


def striped(idx):
    return np.tile(np.asarray(idx).reshape(-1, 16).T, (8, 1)).astype(np.uint16)


def unstriped(offs):
    return offs[:16].T.reshape(-1).astype(np.int64)


E2M1 = np.array([0.0, 0.5, 1.0, 1.5, 2.0, 3.0, 4.0, 6.0, -0.0, -0.5, -1.0, -1.5, -2.0, -3.0, -4.0, -6.0])


def pack_weight(w, fmt):
    k, n = w.shape
    w = f64(np.asarray(w, np.float32).astype(ml_dtypes.bfloat16)).reshape(k // 32, 32, n)
    amax = np.abs(w).max(1)
    if fmt in ("e4m3", "e5m2"):
        byte = np.frexp(amax)[1] - 1 + 127 - (7 if fmt == "e4m3" else 14)
    else:
        mant, ex = np.frexp(amax / 6.0)
        byte = np.where(mant > 0.5, ex, ex - 1) + 127
    byte = np.clip(np.where(amax > 0, byte, 1), 1, 254)
    scaled = (w * np.exp2(127.0 - byte)[:, None, :]).reshape(k, n).astype(np.float32)
    by_word = np.ascontiguousarray(scaled.reshape(k // 512, 128, 4, n).transpose(0, 1, 3, 2))
    if fmt in ("e4m3", "e5m2"):
        words = by_word.astype(ml_dtypes.float8_e4m3fn if fmt == "e4m3" else ml_dtypes.float8_e5m2).view(np.uint8)
    else:
        c = by_word.astype(ml_dtypes.float4_e2m1fn).view(np.uint8) & 0xF
        words = (c[..., 0::2] | (c[..., 1::2] << 4)).reshape(k // 512, 128, 2 * n)
    return np.ascontiguousarray(words), np.ascontiguousarray(byte.astype(np.uint8).reshape(k // 512, 16, n))


def unpack_weight(words, scales, fmt):
    g, _, n = scales.shape
    words = np.ascontiguousarray(words).reshape(g, 128, n, -1)
    if fmt in ("e4m3", "e5m2"):
        vals = words.view(ml_dtypes.float8_e4m3fn if fmt == "e4m3" else ml_dtypes.float8_e5m2).astype(np.float64)
    else:
        nib = np.empty((g, 128, n, 4), np.uint8)
        nib[..., 0::2] = words & 0xF
        nib[..., 1::2] = words >> 4
        vals = E2M1[nib]
    vals = vals * np.repeat(np.exp2(scales.astype(np.float64) - 127.0), 8, axis=1)[..., None]
    return vals.transpose(0, 1, 3, 2).reshape(g * 512, n)


K, T, Z, J, R, N, L = 512, 1024, 1024, 256, 512, 256, 512


def setup_inputs():
    n = np.random.standard_normal
    idx = np.random.permutation(T)[:J]
    idx2 = np.random.permutation(Z)[:J]
    idx3 = np.random.permutation(J)[:J]
    idx4 = np.random.permutation(J)[:J]
    fk = mx_kscale(K)
    fr = mx_kscale(R)
    fl = mx_kscale(L)
    xtp = pack_weight(n((K, T)) / fk[:, None], "e5m2")
    xop = pack_weight(n((K, Z)) / fk[:, None], "e4m3")
    wp = pack_weight(n((K, R)) * 1 / np.sqrt(K) * fk[:, None] * fr, "e2m1")
    w2p = pack_weight(n((K, R)) * 1 / np.sqrt(K) * fk[:, None] * fr, "e5m2")
    wbp = pack_weight(n((R, N)) * 1 / np.sqrt(R) / fr[:, None], "e2m1")
    sxp = pack_weight(n((L, J)) / fl[:, None], "e4m3")
    wsp = pack_weight(n((L, N)) * 1 / np.sqrt(L) * fl[:, None], "e2m1")
    return {
        "xt_words": xtp[0],
        "xt_scales": xtp[1],
        "xo_words": xop[0],
        "xo_scales": xop[1],
        "w_words": wp[0],
        "w_scales": wp[1],
        "w2_words": w2p[0],
        "w2_scales": w2p[1],
        "wb_words": wbp[0],
        "wb_scales": wbp[1],
        "sx_words": sxp[0],
        "sx_scales": sxp[1],
        "ws_words": wsp[0],
        "ws_scales": wsp[1],
        "offs": striped(idx),
        "offs2": striped(idx2),
        "offs3": striped(idx3),
        "offs4": striped(idx4),
    }


def reference(xt_words, xt_scales, xo_words, xo_scales, w_words, w_scales, w2_words, w2_scales, wb_words, wb_scales, sx_words, sx_scales, ws_words, ws_scales, offs, offs2, offs3, offs4):
    idx = unstriped(offs)
    idx2 = unstriped(offs2)
    idx3 = unstriped(offs3)
    idx4 = unstriped(offs4)
    xtu = unpack_weight(xt_words, xt_scales, "e5m2")
    xou = unpack_weight(xo_words, xo_scales, "e4m3")
    wu = unpack_weight(w_words, w_scales, "e2m1")
    w2u = unpack_weight(w2_words, w2_scales, "e5m2")
    wbu = unpack_weight(wb_words, wb_scales, "e2m1")
    sxu = unpack_weight(sx_words, sx_scales, "e4m3")
    wsu = unpack_weight(ws_words, ws_scales, "e2m1")
    xtidxg = xtu[:, idx]
    xoidx2g = xou[:, idx2]
    a = wu.T @ xtidxg + w2u.T @ xoidx2g
    b = w2u.T @ xtidxg + wu.T @ xoidx2g
    hid = np.maximum(np.abs(a[:, idx3] - a[:, idx4]), b)
    hidq = mxq(hid, 0, "e4m3")
    y = wbu.T @ hidq + wsu.T @ sxu
    return y

@@ -1,0 +1,182 @@
+from contextlib import ExitStack
+
+import concourse.mybir as mybir
+
+K, T, Z, J, R, N, L = 512, 1024, 1024, 256, 512, 256, 512
+FLOPS = 2 * J * (4 * K * R + R * N + L * N)
+
+F32 = mybir.dt.float32
+BF16 = mybir.dt.bfloat16
+I32 = mybir.dt.int32
+U32 = mybir.dt.uint32
+U16 = mybir.dt.uint16
+U8 = mybir.dt.uint8
+E4M3 = mybir.dt.float8_e4m3fn_x4
+E5M2 = mybir.dt.float8_e5m2_x4
+E2M1 = mybir.dt.float4_e2m1fn_x4
+ALU = mybir.AluOpType
+ACT = mybir.ActivationFunctionType
+
+P = 128
+PACK = 4
+ROWS = 16
+HALF = J // 2
+
+
+def tile_list_betweentwo_crossed_skip_plain_kernel(
+    tc, xt_words, xt_scales, xo_words, xo_scales, w_words, w_scales, w2_words, w2_scales,
+    wb_words, wb_scales, sx_words, sx_scales, ws_words, ws_scales, offs, offs2, offs3, offs4, out,
+):
+    nc = tc.nc
+    with ExitStack() as ctx:
+        sb = ctx.enter_context(tc.tile_pool(name="sb", bufs=1))
+        ps = ctx.enter_context(tc.psum_pool(name="ps", bufs=1))
+
+        def tile(name, shape, dtype, tag=None):
+            return sb.tile(shape, dtype, name=name, tag=tag or name, align_bytes=64)
+
+        def words_of(dram):
+            return dram[0].rearrange("p n t -> p (n t)").bitcast(I32)
+
+        def spread(plane, rows):
+            for q in range(4):
+                nc.sync.dma_start(out=plane[32 * q : 32 * q + 4, :].bitcast(I32), in_=rows[4 * q : 4 * q + 4, :].bitcast(I32))
+
+        idx1 = sb.tile([P, J // 16], U16, name="idx1")
+        idx2 = sb.tile([P, J // 16], U16, name="idx2")
+        idx3 = sb.tile([P, J // 16], U16, name="idx3")
+        idx4 = sb.tile([P, J // 16], U16, name="idx4")
+        xt_w = tile("xt_w", [P, T], I32)
+        xo_w = tile("xo_w", [P, Z], I32)
+        xt_s = tile("xt_s", [P, T], U8)
+        xo_s = tile("xo_s", [P, Z], U8)
+        w_raw = tile("w_raw", [P, 2 * R], U8)
+        w2_raw = tile("w2_raw", [P, R], I32)
+        ww_s = tile("ww_s", [P, 2 * R], U8)
+
+        nc.vector.memset(xt_s[:].bitcast(I32), 0)
+        nc.vector.memset(xo_s[:].bitcast(I32), 0)
+        nc.gpsimd.memset(ww_s[:].bitcast(I32), 0)
+
+        nc.sync.dma_start(idx1[:], offs)
+        nc.sync.dma_start(idx2[:], offs2)
+        nc.sync.dma_start(out=xt_s[0:ROWS, :].bitcast(I32), in_=xt_scales[0].bitcast(I32))
+        nc.sync.dma_start(out=xo_s[0:ROWS, :].bitcast(I32), in_=xo_scales[0].bitcast(I32))
+        nc.scalar.dma_start(out=ww_s[0:ROWS, 0:R].bitcast(I32), in_=w_scales[0].bitcast(I32))
+        nc.scalar.dma_start(out=ww_s[0:ROWS, R : 2 * R].bitcast(I32), in_=w2_scales[0].bitcast(I32))
+        nc.sync.dma_start(out=xt_w[:], in_=words_of(xt_words))
+        nc.sync.dma_start(out=xo_w[:], in_=words_of(xo_words))
+        nc.sync.dma_start(out=w_raw[:].bitcast(I32), in_=w_words[0].bitcast(I32))
+        nc.sync.dma_start(out=w2_raw[:], in_=words_of(w2_words))
+        nc.sync.dma_start(idx4[:], offs4)
+        nc.sync.dma_start(idx3[:], offs3)
+
+        xt_gs = tile("xt_gs", [P, J], U8)
+        xo_gs = tile("xo_gs", [P, J], U8)
+        plane1 = tile("plane1", [P, 2 * J + 2 * R], U8)
+        rows1 = tile("rows1", [P, 2 * J + 2 * R], U8)
+        nc.vector.tensor_copy(xt_gs[:], xt_s[:].indirect(idx1[:]))
+        nc.vector.tensor_copy(xo_gs[:], xo_s[:].indirect(idx2[:]))
+        nc.gpsimd.tensor_copy(
+            out=rows1[:, 2 * J :].rearrange("p (u t m) -> p u t m", u=2, t=PACK),
+            in_=ww_s[:].rearrange("p (u m t) -> p u t m", u=2, t=PACK),
+        )
+        nc.vector.tensor_copy(out=rows1[:, 0:J].bitcast(I32), in_=xt_gs[:].bitcast(I32))
+        nc.vector.tensor_copy(out=rows1[:, J : 2 * J].bitcast(I32), in_=xo_gs[:].bitcast(I32))
+        spread(plane1, rows1)
+
+
+        xt_g = tile("xt_g", [P, J], U32)
+        xo_g = tile("xo_g", [P, J], U32)
+        w_p = tile("w_p", [P, 2 * R], U8)
+        w2_p = tile("w2_p", [P, R], I32)
+        nc.vector.tensor_copy(xt_g[:], xt_w[:].bitcast(U32).indirect(idx1[:]))
+        nc.vector.tensor_copy(xo_g[:], xo_w[:].bitcast(U32).indirect(idx2[:]))
+        nc.vector.tensor_copy(
+            out=w_p[:].bitcast(U16).rearrange("p (t m) -> p m t", t=PACK),
+            in_=w_raw[:].bitcast(U16).rearrange("p (m t) -> p m t", t=PACK),
+        )
+        nc.vector.tensor_copy(
+            out=w2_p[:].rearrange("p (t m) -> p m t", t=PACK),
+            in_=w2_raw[:].rearrange("p (m t) -> p m t", t=PACK),
+        )
+
+        late = tile("late", [P, 6 * N + 5 * J], U8, tag="ww_s")
+        rows2 = late[:, 0 : 2 * N + J]
+        plane2 = tile("plane2", [P, 2 * N + J], U8)
+        nc.sync.dma_start(out=rows2[0:ROWS, 0:N].bitcast(I32), in_=wb_scales[0].bitcast(I32))
+        nc.sync.dma_start(out=rows2[0:ROWS, N : 2 * N].bitcast(I32), in_=ws_scales[0].bitcast(I32))
+        nc.sync.dma_start(out=rows2[0:ROWS, 2 * N : 2 * N + J].bitcast(I32), in_=sx_scales[0].bitcast(I32))
+        out_w = late[:, 2 * N + J :]
+        wb_w = out_w[:, 0 : 2 * N]
+        ws_w = out_w[:, 2 * N : 4 * N]
+        sx_w = out_w[:, 4 * N :].bitcast(I32)
+        nc.sync.dma_start(out=ws_w.bitcast(I32), in_=ws_words[0].bitcast(I32))
+        nc.sync.dma_start(out=wb_w.bitcast(I32), in_=wb_words[0].bitcast(I32))
+        nc.sync.dma_start(out=sx_w, in_=words_of(sx_words))
+        spread(plane2, rows2)
+
+        def w_side(t):
+            return w_p[:, 2 * P * t : 2 * P * (t + 1)].bitcast(E2M1), plane1[:, 2 * J + P * t : 2 * J + P * (t + 1)]
+
+        def w2_side(t):
+            return w2_p[:, P * t : P * (t + 1)].bitcast(E5M2), plane1[:, 2 * J + R + P * t : 2 * J + R + P * (t + 1)]
+
+        def xt_side(c0, c1):
+            return xt_g[:, c0:c1].bitcast(E5M2), plane1[:, c0:c1]
+
+        def xo_side(c0, c1):
+            return xo_g[:, c0:c1].bitcast(E4M3), plane1[:, J + c0 : J + c1]
+
+        def mx(acc, left, right, start, stop):
+            nc.tensor.matmul_mx(out=acc, lhsT=left[0], lhsT_scale=left[1], rhs=right[0], rhs_scale=right[1], start=start, stop=stop)
+
+        a_sb = []
+        for t in range(PACK):
+            a_ps = ps.tile([P, J], F32, name=f"a_ps{t}", tag=f"bank{t}")
+            mx(a_ps[:], w_side(t), xt_side(0, J), True, False)
+            mx(a_ps[:], w2_side(t), xo_side(0, J), False, True)
+            a_t = tile(f"a_sb{t}", [P, J], F32)
+            if t == 1:
+                nc.vector.tensor_copy(out=a_t[:], in_=a_ps[:])
+            else:
+                nc.scalar.copy(out=a_t[:], in_=a_ps[:])
+            a_sb.append(a_t)
+
+        for h in range(2):
+            c0, c1 = h * HALF, (h + 1) * HALF
+            cols = slice(h * HALF // 16, (h + 1) * HALF // 16)
+            b_ps = ps.tile([P, PACK, HALF], F32, name=f"b_ps{h}", tag=f"b_bank{h}")
+            for t in range(PACK):
+                mx(b_ps[:, t, :], w2_side(t), xt_side(c0, c1), True, False)
+                mx(b_ps[:, t, :], w_side(t), xo_side(c0, c1), False, True)
+            y_ps = []
+            for nb in range(2):
+                y = ps.tile([P, HALF], F32, name=f"y_ps{h}{nb}", tag=f"bank{2 * h + nb}")
+                mx(y[:], (ws_w[:, 2 * P * nb : 2 * P * (nb + 1)].bitcast(E2M1), plane2[:, N + P * nb : N + P * (nb + 1)]),
+                   (sx_w[:, c0:c1].bitcast(E4M3), plane2[:, 2 * N + c0 : 2 * N + c1]), True, False)
+                y_ps.append(y)
+
+            diff = tile(f"diff{h}", [P, PACK, HALF], F32)
+            for t in range(PACK):
+                other = tile(f"other{h}{t}", [P, HALF], F32, tag=f"other{t}")
+                nc.scalar.activation(other[:], a_sb[t][:].indirect(idx4[:, cols]), ACT.Copy)
+                nc.vector.tensor_tensor(diff[:, t, :], a_sb[t][:].indirect(idx3[:, cols]), other[:], ALU.subtract)
+            mag = tile(f"mag{h}", [P, PACK, HALF], F32)
+            nc.scalar.activation(mag[:, 0:3, :], diff[:, 0:3, :], ACT.Abs)
+            nc.scalar.activation(mag[:, 3, :], diff[:, 3, :], ACT.Abs)
+            hid = tile(f"hid{h}", [P, HALF, PACK], BF16)
+            nc.vector.tensor_tensor(hid[:], mag[:].rearrange("p t j -> p j t"), b_ps[:].rearrange("p t j -> p j t"), ALU.max)
+            hid_w = tile(f"hid_w{h}", [P, HALF], U32)
+            hid_s = tile(f"hid_s{h}", [P, HALF], U8)
+            nc.vector.quantize_mx(out=hid_w[:].bitcast(E4M3), scales=hid_s[:], in_=hid[:].rearrange("p j t -> p (j t)"))
+            for nb in range(2):
+                mx(y_ps[nb][:], (wb_w[:, 2 * P * nb : 2 * P * (nb + 1)].bitcast(E2M1), plane2[:, P * nb : P * (nb + 1)]),
+                   (hid_w[:].bitcast(E4M3), hid_s[:]), False, True)
+                res = tile(f"res{h}{nb}", [P, HALF], F32)
+                if nb == 0:
+                    nc.scalar.copy(out=res[:], in_=y_ps[nb][:])
+                    nc.scalar.dma_start(out=out[P * nb : P * (nb + 1), c0:c1], in_=res[:])
+                else:
+                    nc.vector.tensor_copy(out=res[:], in_=y_ps[nb][:])
+                    nc.sync.dma_start(out=out[P * nb : P * (nb + 1), c0:c1], in_=res[:])

@@ -38,9 +38,17 @@ def tile_list_betweentwo_crossed_skip_plain_kernel(
         def words_of(dram):
             return dram[0].rearrange("p n t -> p (n t)").bitcast(I32)
 
-        def spread(plane, rows):
+        def spread(plane, first):
             for q in range(4):
-                nc.sync.dma_start(out=plane[32 * q : 32 * q + 4, :].bitcast(I32), in_=rows[4 * q : 4 * q + 4, :].bitcast(I32))
+                if first + 4 * q != 32 * q:
+                    nc.sync.dma_start(
+                        out=plane[32 * q : 32 * q + 4, :].bitcast(I32),
+                        in_=plane[first + 4 * q : first + 4 * q + 4, :].bitcast(I32),
+                    )
+
+        def clear(engine, staged):
+            for lo, hi in ((0, ROWS), (32, 64), (64, P)):
+                engine.memset(staged[lo:hi, :].bitcast(I32), 0)
 
         idx1 = sb.tile([P, J // 16], U16, name="idx1")
         idx2 = sb.tile([P, J // 16], U16, name="idx2")
@@ -54,59 +62,57 @@ def tile_list_betweentwo_crossed_skip_plain_kernel(
         w2_raw = tile("w2_raw", [P, R], I32)
         ww_s = tile("ww_s", [P, 2 * R], U8)
 
-        nc.vector.memset(xt_s[:].bitcast(I32), 0)
-        nc.vector.memset(xo_s[:].bitcast(I32), 0)
-        nc.gpsimd.memset(ww_s[:].bitcast(I32), 0)
-
+        clear(nc.vector, xt_s)
+        clear(nc.vector, xo_s)
+        clear(nc.gpsimd, ww_s)
+        live = slice(ROWS, 2 * ROWS)
         nc.sync.dma_start(idx1[:], offs)
+        nc.scalar.dma_start(out=ww_s[live, 0:R].bitcast(I32), in_=w_scales[0].bitcast(I32))
+        nc.sync.dma_start(out=xt_s[live, :].bitcast(I32), in_=xt_scales[0].bitcast(I32))
+        nc.scalar.dma_start(out=ww_s[live, R : 2 * R].bitcast(I32), in_=w2_scales[0].bitcast(I32))
         nc.sync.dma_start(idx2[:], offs2)
-        nc.sync.dma_start(out=xt_s[0:ROWS, :].bitcast(I32), in_=xt_scales[0].bitcast(I32))
-        nc.sync.dma_start(out=xo_s[0:ROWS, :].bitcast(I32), in_=xo_scales[0].bitcast(I32))
-        nc.scalar.dma_start(out=ww_s[0:ROWS, 0:R].bitcast(I32), in_=w_scales[0].bitcast(I32))
-        nc.scalar.dma_start(out=ww_s[0:ROWS, R : 2 * R].bitcast(I32), in_=w2_scales[0].bitcast(I32))
+        nc.scalar.dma_start(out=w2_raw[:], in_=words_of(w2_words))
+        nc.sync.dma_start(out=xo_s[live, :].bitcast(I32), in_=xo_scales[0].bitcast(I32))
         nc.sync.dma_start(out=xt_w[:], in_=words_of(xt_words))
-        nc.sync.dma_start(out=xo_w[:], in_=words_of(xo_words))
         nc.sync.dma_start(out=w_raw[:].bitcast(I32), in_=w_words[0].bitcast(I32))
-        nc.sync.dma_start(out=w2_raw[:], in_=words_of(w2_words))
-        nc.sync.dma_start(idx4[:], offs4)
-        nc.sync.dma_start(idx3[:], offs3)
+        nc.sync.dma_start(out=xo_w[:], in_=words_of(xo_words))
 
         xt_gs = tile("xt_gs", [P, J], U8)
         xo_gs = tile("xo_gs", [P, J], U8)
         plane1 = tile("plane1", [P, 2 * J + 2 * R], U8)
-        rows1 = tile("rows1", [P, 2 * J + 2 * R], U8)
         nc.vector.tensor_copy(xt_gs[:], xt_s[:].indirect(idx1[:]))
         nc.vector.tensor_copy(xo_gs[:], xo_s[:].indirect(idx2[:]))
         nc.gpsimd.tensor_copy(
-            out=rows1[:, 2 * J :].rearrange("p (u t m) -> p u t m", u=2, t=PACK),
+            out=plane1[:, 2 * J :].rearrange("p (u t m) -> p u t m", u=2, t=PACK),
             in_=ww_s[:].rearrange("p (u m t) -> p u t m", u=2, t=PACK),
         )
-        nc.vector.tensor_copy(out=rows1[:, 0:J].bitcast(I32), in_=xt_gs[:].bitcast(I32))
-        nc.vector.tensor_copy(out=rows1[:, J : 2 * J].bitcast(I32), in_=xo_gs[:].bitcast(I32))
-        spread(plane1, rows1)
+        nc.vector.tensor_copy(out=plane1[:, 0:J].bitcast(I32), in_=xt_gs[:].bitcast(I32))
+        nc.vector.tensor_copy(out=plane1[:, J : 2 * J].bitcast(I32), in_=xo_gs[:].bitcast(I32))
+        spread(plane1, ROWS)
+        nc.sync.dma_start(idx4[:], offs4)
+        nc.sync.dma_start(idx3[:], offs3)
 
 
         xt_g = tile("xt_g", [P, J], U32)
         xo_g = tile("xo_g", [P, J], U32)
         w_p = tile("w_p", [P, 2 * R], U8)
-        w2_p = tile("w2_p", [P, R], I32)
+        w2_p = tile("w2_p", [P, R], U32)
         nc.vector.tensor_copy(xt_g[:], xt_w[:].bitcast(U32).indirect(idx1[:]))
         nc.vector.tensor_copy(xo_g[:], xo_w[:].bitcast(U32).indirect(idx2[:]))
-        nc.vector.tensor_copy(
+        nc.scalar.copy(
             out=w_p[:].bitcast(U16).rearrange("p (t m) -> p m t", t=PACK),
             in_=w_raw[:].bitcast(U16).rearrange("p (m t) -> p m t", t=PACK),
         )
-        nc.vector.tensor_copy(
+        nc.scalar.copy(
             out=w2_p[:].rearrange("p (t m) -> p m t", t=PACK),
-            in_=w2_raw[:].rearrange("p (m t) -> p m t", t=PACK),
+            in_=w2_raw[:].bitcast(U32).rearrange("p (m t) -> p m t", t=PACK),
         )
 
-        late = tile("late", [P, 6 * N + 5 * J], U8, tag="ww_s")
-        rows2 = late[:, 0 : 2 * N + J]
-        plane2 = tile("plane2", [P, 2 * N + J], U8)
-        nc.sync.dma_start(out=rows2[0:ROWS, 0:N].bitcast(I32), in_=wb_scales[0].bitcast(I32))
-        nc.sync.dma_start(out=rows2[0:ROWS, N : 2 * N].bitcast(I32), in_=ws_scales[0].bitcast(I32))
-        nc.sync.dma_start(out=rows2[0:ROWS, 2 * N : 2 * N + J].bitcast(I32), in_=sx_scales[0].bitcast(I32))
+        late = tile("late", [P, 6 * N + 5 * J], U8, tag="xt_w")
+        plane2 = late[:, 0 : 2 * N + J]
+        nc.sync.dma_start(out=plane2[0:ROWS, 0:N].bitcast(I32), in_=wb_scales[0].bitcast(I32))
+        nc.sync.dma_start(out=plane2[0:ROWS, N : 2 * N].bitcast(I32), in_=ws_scales[0].bitcast(I32))
+        nc.sync.dma_start(out=plane2[0:ROWS, 2 * N : 2 * N + J].bitcast(I32), in_=sx_scales[0].bitcast(I32))
         out_w = late[:, 2 * N + J :]
         wb_w = out_w[:, 0 : 2 * N]
         ws_w = out_w[:, 2 * N : 4 * N]
@@ -114,7 +120,7 @@ def tile_list_betweentwo_crossed_skip_plain_kernel(
         nc.sync.dma_start(out=ws_w.bitcast(I32), in_=ws_words[0].bitcast(I32))
         nc.sync.dma_start(out=wb_w.bitcast(I32), in_=wb_words[0].bitcast(I32))
         nc.sync.dma_start(out=sx_w, in_=words_of(sx_words))
-        spread(plane2, rows2)
+        spread(plane2, 0)
 
         def w_side(t):
             return w_p[:, 2 * P * t : 2 * P * (t + 1)].bitcast(E2M1), plane1[:, 2 * J + P * t : 2 * J + P * (t + 1)]
@@ -131,42 +137,50 @@ def tile_list_betweentwo_crossed_skip_plain_kernel(
         def mx(acc, left, right, start, stop):
             nc.tensor.matmul_mx(out=acc, lhsT=left[0], lhsT_scale=left[1], rhs=right[0], rhs_scale=right[1], start=start, stop=stop)
 
-        a_sb = []
+        a_ps = [ps.tile([P, J], F32, name=f"a_ps{t}", tag=f"bank{t}") for t in range(PACK)]
+        a_sb = [tile(f"a_sb{t}", [P, J], F32) for t in range(PACK)]
         for t in range(PACK):
-            a_ps = ps.tile([P, J], F32, name=f"a_ps{t}", tag=f"bank{t}")
-            mx(a_ps[:], w_side(t), xt_side(0, J), True, False)
-            mx(a_ps[:], w2_side(t), xo_side(0, J), False, True)
-            a_t = tile(f"a_sb{t}", [P, J], F32)
-            if t == 1:
-                nc.vector.tensor_copy(out=a_t[:], in_=a_ps[:])
-            else:
-                nc.scalar.copy(out=a_t[:], in_=a_ps[:])
-            a_sb.append(a_t)
+            mx(a_ps[t][:], w_side(t), xt_side(0, J), True, False)
+            mx(a_ps[t][:], w2_side(t), xo_side(0, J), False, True)
+        b_ps = [ps.tile([P, PACK, HALF], F32, name=f"b_ps{h}", tag=f"b_bank{h}") for h in range(2)]
+        for h in range(2):
+            for t in range(PACK):
+                mx(b_ps[h][:, t, :], w2_side(t), xt_side(h * HALF, (h + 1) * HALF), True, False)
+                mx(b_ps[h][:, t, :], w_side(t), xo_side(h * HALF, (h + 1) * HALF), False, True)
+
+        diff = [tile(f"diff{h}", [P, PACK, HALF], F32) for h in range(2)]
+
+        def difference(h, t):
+            cols = slice(h * HALF // 16, (h + 1) * HALF // 16)
+            other = tile(f"other{h}{t}", [P, HALF], F32)
+            nc.scalar.activation(other[:], a_sb[t][:].indirect(idx4[:, cols]), ACT.Copy)
+            nc.vector.tensor_tensor(diff[h][:, t, :], a_sb[t][:].indirect(idx3[:, cols]), other[:], ALU.subtract)
+
+        nc.vector.tensor_copy(out=a_sb[0][:], in_=a_ps[0][:])
+        nc.vector.tensor_copy(out=a_sb[1][:], in_=a_ps[1][:])
+        difference(0, 0)
+        difference(1, 0)
+        nc.scalar.copy(out=a_sb[2][:], in_=a_ps[2][:])
+        difference(0, 1)
+        nc.scalar.copy(out=a_sb[3][:], in_=a_ps[3][:])
+        difference(0, 2)
+        difference(0, 3)
+        for t in range(1, PACK):
+            difference(1, t)
 
         for h in range(2):
             c0, c1 = h * HALF, (h + 1) * HALF
-            cols = slice(h * HALF // 16, (h + 1) * HALF // 16)
-            b_ps = ps.tile([P, PACK, HALF], F32, name=f"b_ps{h}", tag=f"b_bank{h}")
-            for t in range(PACK):
-                mx(b_ps[:, t, :], w2_side(t), xt_side(c0, c1), True, False)
-                mx(b_ps[:, t, :], w_side(t), xo_side(c0, c1), False, True)
             y_ps = []
             for nb in range(2):
                 y = ps.tile([P, HALF], F32, name=f"y_ps{h}{nb}", tag=f"bank{2 * h + nb}")
                 mx(y[:], (ws_w[:, 2 * P * nb : 2 * P * (nb + 1)].bitcast(E2M1), plane2[:, N + P * nb : N + P * (nb + 1)]),
                    (sx_w[:, c0:c1].bitcast(E4M3), plane2[:, 2 * N + c0 : 2 * N + c1]), True, False)
                 y_ps.append(y)
-
-            diff = tile(f"diff{h}", [P, PACK, HALF], F32)
-            for t in range(PACK):
-                other = tile(f"other{h}{t}", [P, HALF], F32, tag=f"other{t}")
-                nc.scalar.activation(other[:], a_sb[t][:].indirect(idx4[:, cols]), ACT.Copy)
-                nc.vector.tensor_tensor(diff[:, t, :], a_sb[t][:].indirect(idx3[:, cols]), other[:], ALU.subtract)
             mag = tile(f"mag{h}", [P, PACK, HALF], F32)
-            nc.scalar.activation(mag[:, 0:3, :], diff[:, 0:3, :], ACT.Abs)
-            nc.scalar.activation(mag[:, 3, :], diff[:, 3, :], ACT.Abs)
+            nc.scalar.activation(mag[:, 0:3, :], diff[h][:, 0:3, :], ACT.Abs)
+            nc.scalar.activation(mag[:, 3, :], diff[h][:, 3, :], ACT.Abs)
             hid = tile(f"hid{h}", [P, HALF, PACK], BF16)
-            nc.vector.tensor_tensor(hid[:], mag[:].rearrange("p t j -> p j t"), b_ps[:].rearrange("p t j -> p j t"), ALU.max)
+            nc.vector.tensor_tensor(hid[:], mag[:].rearrange("p t j -> p j t"), b_ps[h][:].rearrange("p t j -> p j t"), ALU.max)
             hid_w = tile(f"hid_w{h}", [P, HALF], U32)
             hid_s = tile(f"hid_s{h}", [P, HALF], U8)
             nc.vector.quantize_mx(out=hid_w[:].bitcast(E4M3), scales=hid_s[:], in_=hid[:].rearrange("p j t -> p (j t)"))

@@ -46,9 +46,6 @@ def tile_list_betweentwo_crossed_skip_plain_kernel(
                         in_=plane[first + 4 * q : first + 4 * q + 4, :].bitcast(I32),
                     )
 
-        def clear(engine, staged):
-            for lo, hi in ((0, ROWS), (32, 64), (64, P)):
-                engine.memset(staged[lo:hi, :].bitcast(I32), 0)
 
         idx1 = sb.tile([P, J // 16], U16, name="idx1")
         idx2 = sb.tile([P, J // 16], U16, name="idx2")
@@ -62,10 +59,9 @@ def tile_list_betweentwo_crossed_skip_plain_kernel(
         w2_raw = tile("w2_raw", [P, R], I32)
         ww_s = tile("ww_s", [P, 2 * R], U8)
 
-        clear(nc.vector, xt_s)
-        clear(nc.vector, xo_s)
-        clear(nc.gpsimd, ww_s)
-        live = slice(ROWS, 2 * ROWS)
+        for staged in (ww_s, xt_s, xo_s):
+            nc.vector.memset(staged[0 : P - ROWS, :].bitcast(I32), 0)
+        live = slice(P - ROWS, P)
         nc.sync.dma_start(idx1[:], offs)
         nc.scalar.dma_start(out=ww_s[live, 0:R].bitcast(I32), in_=w_scales[0].bitcast(I32))
         nc.sync.dma_start(out=xt_s[live, :].bitcast(I32), in_=xt_scales[0].bitcast(I32))
@@ -82,13 +78,13 @@ def tile_list_betweentwo_crossed_skip_plain_kernel(
         plane1 = tile("plane1", [P, 2 * J + 2 * R], U8)
         nc.vector.tensor_copy(xt_gs[:], xt_s[:].indirect(idx1[:]))
         nc.vector.tensor_copy(xo_gs[:], xo_s[:].indirect(idx2[:]))
-        nc.gpsimd.tensor_copy(
+        nc.vector.tensor_copy(
             out=plane1[:, 2 * J :].rearrange("p (u t m) -> p u t m", u=2, t=PACK),
             in_=ww_s[:].rearrange("p (u m t) -> p u t m", u=2, t=PACK),
         )
         nc.vector.tensor_copy(out=plane1[:, 0:J].bitcast(I32), in_=xt_gs[:].bitcast(I32))
         nc.vector.tensor_copy(out=plane1[:, J : 2 * J].bitcast(I32), in_=xo_gs[:].bitcast(I32))
-        spread(plane1, ROWS)
+        spread(plane1, P - ROWS)
         nc.sync.dma_start(idx4[:], offs4)
         nc.sync.dma_start(idx3[:], offs3)
 
@@ -100,12 +96,12 @@ def tile_list_betweentwo_crossed_skip_plain_kernel(
         nc.vector.tensor_copy(xt_g[:], xt_w[:].bitcast(U32).indirect(idx1[:]))
         nc.vector.tensor_copy(xo_g[:], xo_w[:].bitcast(U32).indirect(idx2[:]))
         nc.scalar.copy(
-            out=w_p[:].bitcast(U16).rearrange("p (t m) -> p m t", t=PACK),
-            in_=w_raw[:].bitcast(U16).rearrange("p (m t) -> p m t", t=PACK),
+            out=w_p[:].bitcast(U16).rearrange("p (t m) -> p t m", t=PACK),
+            in_=w_raw[:].bitcast(U16).rearrange("p (m t) -> p t m", t=PACK),
         )
         nc.scalar.copy(
-            out=w2_p[:].rearrange("p (t m) -> p m t", t=PACK),
-            in_=w2_raw[:].bitcast(U32).rearrange("p (m t) -> p m t", t=PACK),
+            out=w2_p[:].rearrange("p (t m) -> p t m", t=PACK),
+            in_=w2_raw[:].bitcast(U32).rearrange("p (m t) -> p t m", t=PACK),
         )
 
         late = tile("late", [P, 6 * N + 5 * J], U8, tag="xt_w")
@@ -176,11 +172,10 @@ def tile_list_betweentwo_crossed_skip_plain_kernel(
                 mx(y[:], (ws_w[:, 2 * P * nb : 2 * P * (nb + 1)].bitcast(E2M1), plane2[:, N + P * nb : N + P * (nb + 1)]),
                    (sx_w[:, c0:c1].bitcast(E4M3), plane2[:, 2 * N + c0 : 2 * N + c1]), True, False)
                 y_ps.append(y)
-            mag = tile(f"mag{h}", [P, PACK, HALF], F32)
-            nc.scalar.activation(mag[:, 0:3, :], diff[h][:, 0:3, :], ACT.Abs)
-            nc.scalar.activation(mag[:, 3, :], diff[h][:, 3, :], ACT.Abs)
+            mag = tile(f"mag{h}", [P, HALF, PACK], F32)
+            nc.scalar.activation(mag[:], diff[h][:].rearrange("p t j -> p j t"), ACT.Abs)
             hid = tile(f"hid{h}", [P, HALF, PACK], BF16)
-            nc.vector.tensor_tensor(hid[:], mag[:].rearrange("p t j -> p j t"), b_ps[h][:].rearrange("p t j -> p j t"), ALU.max)
+            nc.vector.tensor_tensor(hid[:], mag[:], b_ps[h][:].rearrange("p t j -> p j t"), ALU.max)
             hid_w = tile(f"hid_w{h}", [P, HALF], U32)
             hid_s = tile(f"hid_s{h}", [P, HALF], U8)
             nc.vector.quantize_mx(out=hid_w[:].bitcast(E4M3), scales=hid_s[:], in_=hid[:].rearrange("p j t -> p (j t)"))

@@ -19,7 +19,9 @@ ACT = mybir.ActivationFunctionType
 
 P = 128
 PACK = 4
+QUAD = 32
 ROWS = 16
+GROUP = 16
 HALF = J // 2
 
 
@@ -38,19 +40,23 @@ def tile_list_betweentwo_crossed_skip_plain_kernel(
         def words_of(dram):
             return dram[0].rearrange("p n t -> p (n t)").bitcast(I32)
 
-        def spread(plane, first):
-            for q in range(4):
-                if first + 4 * q != 32 * q:
-                    nc.sync.dma_start(
-                        out=plane[32 * q : 32 * q + 4, :].bitcast(I32),
+        def spread(plane, first, queues):
+            for q in range(P // QUAD):
+                if first + 4 * q != QUAD * q:
+                    queues[q % len(queues)].dma_start(
+                        out=plane[QUAD * q : QUAD * q + 4, :].bitcast(I32),
                         in_=plane[first + 4 * q : first + 4 * q + 4, :].bitcast(I32),
                     )
 
+        def mx(acc, left, right, start, stop):
+            nc.tensor.matmul_mx(
+                out=acc, lhsT=left[0], lhsT_scale=left[1], rhs=right[0], rhs_scale=right[1], start=start, stop=stop
+            )
 
-        idx1 = sb.tile([P, J // 16], U16, name="idx1")
-        idx2 = sb.tile([P, J // 16], U16, name="idx2")
-        idx3 = sb.tile([P, J // 16], U16, name="idx3")
-        idx4 = sb.tile([P, J // 16], U16, name="idx4")
+        idx1 = sb.tile([P, J // GROUP], U16, name="idx1")
+        idx2 = sb.tile([P, J // GROUP], U16, name="idx2")
+        idx3 = sb.tile([P, J // GROUP], U16, name="idx3")
+        idx4 = sb.tile([P, J // GROUP], U16, name="idx4")
         xt_w = tile("xt_w", [P, T], I32)
         xo_w = tile("xo_w", [P, Z], I32)
         xt_s = tile("xt_s", [P, T], U8)
@@ -84,10 +90,9 @@ def tile_list_betweentwo_crossed_skip_plain_kernel(
         )
         nc.vector.tensor_copy(out=plane1[:, 0:J].bitcast(I32), in_=xt_gs[:].bitcast(I32))
         nc.vector.tensor_copy(out=plane1[:, J : 2 * J].bitcast(I32), in_=xo_gs[:].bitcast(I32))
-        spread(plane1, P - ROWS)
+        spread(plane1, P - ROWS, (nc.scalar, nc.sync))
         nc.sync.dma_start(idx4[:], offs4)
         nc.sync.dma_start(idx3[:], offs3)
-
 
         xt_g = tile("xt_g", [P, J], U32)
         xo_g = tile("xo_g", [P, J], U32)
@@ -104,84 +109,94 @@ def tile_list_betweentwo_crossed_skip_plain_kernel(
             in_=w2_raw[:].bitcast(U32).rearrange("p (m t) -> p t m", t=PACK),
         )
 
-        late = tile("late", [P, 6 * N + 5 * J], U8, tag="xt_w")
+        late = tile("late", [P, 2 * N + J + 4 * N + 4 * J], U8, tag="xt_w")
         plane2 = late[:, 0 : 2 * N + J]
         nc.sync.dma_start(out=plane2[0:ROWS, 0:N].bitcast(I32), in_=wb_scales[0].bitcast(I32))
         nc.sync.dma_start(out=plane2[0:ROWS, N : 2 * N].bitcast(I32), in_=ws_scales[0].bitcast(I32))
         nc.sync.dma_start(out=plane2[0:ROWS, 2 * N : 2 * N + J].bitcast(I32), in_=sx_scales[0].bitcast(I32))
-        out_w = late[:, 2 * N + J :]
-        wb_w = out_w[:, 0 : 2 * N]
-        ws_w = out_w[:, 2 * N : 4 * N]
-        sx_w = out_w[:, 4 * N :].bitcast(I32)
+        late_w = late[:, 2 * N + J :]
+        wb_w = late_w[:, 0 : 2 * N]
+        ws_w = late_w[:, 2 * N : 4 * N]
+        sx_w = late_w[:, 4 * N :].bitcast(I32)
         nc.sync.dma_start(out=ws_w.bitcast(I32), in_=ws_words[0].bitcast(I32))
         nc.sync.dma_start(out=wb_w.bitcast(I32), in_=wb_words[0].bitcast(I32))
         nc.sync.dma_start(out=sx_w, in_=words_of(sx_words))
-        spread(plane2, 0)
+        spread(plane2, 0, (nc.sync,))
 
-        def w_side(t):
+        def w_slice(t):
             return w_p[:, 2 * P * t : 2 * P * (t + 1)].bitcast(E2M1), plane1[:, 2 * J + P * t : 2 * J + P * (t + 1)]
 
-        def w2_side(t):
+        def w2_slice(t):
             return w2_p[:, P * t : P * (t + 1)].bitcast(E5M2), plane1[:, 2 * J + R + P * t : 2 * J + R + P * (t + 1)]
 
-        def xt_side(c0, c1):
+        def xt_slots(c0, c1):
             return xt_g[:, c0:c1].bitcast(E5M2), plane1[:, c0:c1]
 
-        def xo_side(c0, c1):
+        def xo_slots(c0, c1):
             return xo_g[:, c0:c1].bitcast(E4M3), plane1[:, J + c0 : J + c1]
 
-        def mx(acc, left, right, start, stop):
-            nc.tensor.matmul_mx(out=acc, lhsT=left[0], lhsT_scale=left[1], rhs=right[0], rhs_scale=right[1], start=start, stop=stop)
+        def wb_block(nb):
+            return wb_w[:, 2 * P * nb : 2 * P * (nb + 1)].bitcast(E2M1), plane2[:, P * nb : P * (nb + 1)]
+
+        def ws_block(nb):
+            return ws_w[:, 2 * P * nb : 2 * P * (nb + 1)].bitcast(E2M1), plane2[:, N + P * nb : N + P * (nb + 1)]
+
+        def sx_slots(c0, c1):
+            return sx_w[:, c0:c1].bitcast(E4M3), plane2[:, 2 * N + c0 : 2 * N + c1]
 
         a_ps = [ps.tile([P, J], F32, name=f"a_ps{t}", tag=f"bank{t}") for t in range(PACK)]
         a_sb = [tile(f"a_sb{t}", [P, J], F32) for t in range(PACK)]
         for t in range(PACK):
-            mx(a_ps[t][:], w_side(t), xt_side(0, J), True, False)
-            mx(a_ps[t][:], w2_side(t), xo_side(0, J), False, True)
+            mx(a_ps[t][:], w_slice(t), xt_slots(0, J), True, False)
+            mx(a_ps[t][:], w2_slice(t), xo_slots(0, J), False, True)
         b_ps = [ps.tile([P, PACK, HALF], F32, name=f"b_ps{h}", tag=f"b_bank{h}") for h in range(2)]
         for h in range(2):
             for t in range(PACK):
-                mx(b_ps[h][:, t, :], w2_side(t), xt_side(h * HALF, (h + 1) * HALF), True, False)
-                mx(b_ps[h][:, t, :], w_side(t), xo_side(h * HALF, (h + 1) * HALF), False, True)
+                mx(b_ps[h][:, t, :], w2_slice(t), xt_slots(h * HALF, (h + 1) * HALF), True, False)
+                mx(b_ps[h][:, t, :], w_slice(t), xo_slots(h * HALF, (h + 1) * HALF), False, True)
 
         diff = [tile(f"diff{h}", [P, PACK, HALF], F32) for h in range(2)]
 
         def difference(h, t):
-            cols = slice(h * HALF // 16, (h + 1) * HALF // 16)
+            cols = slice(h * HALF // GROUP, (h + 1) * HALF // GROUP)
             other = tile(f"other{h}{t}", [P, HALF], F32)
             nc.scalar.activation(other[:], a_sb[t][:].indirect(idx4[:, cols]), ACT.Copy)
             nc.vector.tensor_tensor(diff[h][:, t, :], a_sb[t][:].indirect(idx3[:, cols]), other[:], ALU.subtract)
 
         nc.vector.tensor_copy(out=a_sb[0][:], in_=a_ps[0][:])
         nc.vector.tensor_copy(out=a_sb[1][:], in_=a_ps[1][:])
-        difference(0, 0)
-        difference(1, 0)
-        nc.scalar.copy(out=a_sb[2][:], in_=a_ps[2][:])
-        difference(0, 1)
-        nc.scalar.copy(out=a_sb[3][:], in_=a_ps[3][:])
-        difference(0, 2)
-        difference(0, 3)
-        for t in range(1, PACK):
+        for t in range(2):
+            difference(0, t)
             difference(1, t)
+            nc.scalar.copy(out=a_sb[2 + t][:], in_=a_ps[2 + t][:])
+        for h in range(2):
+            difference(h, 2)
+            difference(h, 3)
 
         for h in range(2):
             c0, c1 = h * HALF, (h + 1) * HALF
             y_ps = []
             for nb in range(2):
                 y = ps.tile([P, HALF], F32, name=f"y_ps{h}{nb}", tag=f"bank{2 * h + nb}")
-                mx(y[:], (ws_w[:, 2 * P * nb : 2 * P * (nb + 1)].bitcast(E2M1), plane2[:, N + P * nb : N + P * (nb + 1)]),
-                   (sx_w[:, c0:c1].bitcast(E4M3), plane2[:, 2 * N + c0 : 2 * N + c1]), True, False)
+                mx(y[:], ws_block(nb), sx_slots(c0, c1), True, False)
                 y_ps.append(y)
-            mag = tile(f"mag{h}", [P, HALF, PACK], F32)
-            nc.scalar.activation(mag[:], diff[h][:].rearrange("p t j -> p j t"), ACT.Abs)
-            hid = tile(f"hid{h}", [P, HALF, PACK], BF16)
-            nc.vector.tensor_tensor(hid[:], mag[:], b_ps[h][:].rearrange("p t j -> p j t"), ALU.max)
+            mag = tile(f"mag{h}", [P, 2, HALF, 2], F32)
+            for u in range(2):
+                nc.scalar.activation(
+                    mag[:, u, :, :], diff[h][:, 2 * u : 2 * u + 2, :].rearrange("p e j -> p j e"), ACT.Abs
+                )
+            hid = tile(f"hid{h}", [P, HALF, 2, 2], BF16)
+            nc.vector.tensor_tensor(
+                hid[:],
+                mag[:].rearrange("p u j e -> p j u e"),
+                b_ps[h][:].rearrange("p (u e) j -> p j u e", e=2),
+                ALU.max,
+            )
             hid_w = tile(f"hid_w{h}", [P, HALF], U32)
             hid_s = tile(f"hid_s{h}", [P, HALF], U8)
-            nc.vector.quantize_mx(out=hid_w[:].bitcast(E4M3), scales=hid_s[:], in_=hid[:].rearrange("p j t -> p (j t)"))
+            nc.vector.quantize_mx(out=hid_w[:].bitcast(E4M3), scales=hid_s[:], in_=hid[:].rearrange("p j u e -> p (j u e)"))
             for nb in range(2):
-                mx(y_ps[nb][:], (wb_w[:, 2 * P * nb : 2 * P * (nb + 1)].bitcast(E2M1), plane2[:, P * nb : P * (nb + 1)]),
-                   (hid_w[:].bitcast(E4M3), hid_s[:]), False, True)
+                mx(y_ps[nb][:], wb_block(nb), (hid_w[:].bitcast(E4M3), hid_s[:]), False, True)
                 res = tile(f"res{h}{nb}", [P, HALF], F32)
                 if nb == 0:
                     nc.scalar.copy(out=res[:], in_=y_ps[nb][:])

from contextlib import ExitStack

import concourse.mybir as mybir

K, T, Z, J, R, N, L = 512, 1024, 1024, 256, 512, 256, 512
FLOPS = 2 * J * (4 * K * R + R * N + L * N)

F32 = mybir.dt.float32
BF16 = mybir.dt.bfloat16
I32 = mybir.dt.int32
U32 = mybir.dt.uint32
U16 = mybir.dt.uint16
U8 = mybir.dt.uint8
E4M3 = mybir.dt.float8_e4m3fn_x4
E5M2 = mybir.dt.float8_e5m2_x4
E2M1 = mybir.dt.float4_e2m1fn_x4
ALU = mybir.AluOpType
ACT = mybir.ActivationFunctionType

P = 128
PACK = 4
QUAD = 32
ROWS = 16
GROUP = 16
HALF = J // 2


def tile_list_betweentwo_crossed_skip_plain_kernel(
    tc, xt_words, xt_scales, xo_words, xo_scales, w_words, w_scales, w2_words, w2_scales,
    wb_words, wb_scales, sx_words, sx_scales, ws_words, ws_scales, offs, offs2, offs3, offs4, out,
):
    nc = tc.nc
    with ExitStack() as ctx:
        sb = ctx.enter_context(tc.tile_pool(name="sb", bufs=1))
        ps = ctx.enter_context(tc.psum_pool(name="ps", bufs=1))

        def tile(name, shape, dtype, tag=None):
            return sb.tile(shape, dtype, name=name, tag=tag or name, align_bytes=64)

        def words_of(dram):
            return dram[0].rearrange("p n t -> p (n t)").bitcast(I32)

        def spread(plane, first, queues):
            for q in range(P // QUAD):
                if first + 4 * q != QUAD * q:
                    queues[q % len(queues)].dma_start(
                        out=plane[QUAD * q : QUAD * q + 4, :].bitcast(I32),
                        in_=plane[first + 4 * q : first + 4 * q + 4, :].bitcast(I32),
                    )

        def mx(acc, left, right, start, stop):
            nc.tensor.matmul_mx(
                out=acc, lhsT=left[0], lhsT_scale=left[1], rhs=right[0], rhs_scale=right[1], start=start, stop=stop
            )

        idx1 = sb.tile([P, J // GROUP], U16, name="idx1")
        idx2 = sb.tile([P, J // GROUP], U16, name="idx2")
        idx3 = sb.tile([P, J // GROUP], U16, name="idx3")
        idx4 = sb.tile([P, J // GROUP], U16, name="idx4")
        xt_w = tile("xt_w", [P, T], I32)
        xo_w = tile("xo_w", [P, Z], I32)
        xt_s = tile("xt_s", [P, T], U8)
        xo_s = tile("xo_s", [P, Z], U8)
        w_raw = tile("w_raw", [P, 2 * R], U8)
        w2_raw = tile("w2_raw", [P, R], I32)
        ww_s = tile("ww_s", [P, 2 * R], U8)

        for staged in (ww_s, xt_s, xo_s):
            nc.vector.memset(staged[0 : P - ROWS, :].bitcast(I32), 0)
        live = slice(P - ROWS, P)
        nc.sync.dma_start(idx1[:], offs)
        nc.scalar.dma_start(out=ww_s[live, 0:R].bitcast(I32), in_=w_scales[0].bitcast(I32))
        nc.sync.dma_start(out=xt_s[live, :].bitcast(I32), in_=xt_scales[0].bitcast(I32))
        nc.scalar.dma_start(out=ww_s[live, R : 2 * R].bitcast(I32), in_=w2_scales[0].bitcast(I32))
        nc.sync.dma_start(idx2[:], offs2)
        nc.scalar.dma_start(out=w2_raw[:], in_=words_of(w2_words))
        nc.sync.dma_start(out=xo_s[live, :].bitcast(I32), in_=xo_scales[0].bitcast(I32))
        nc.sync.dma_start(out=xt_w[:], in_=words_of(xt_words))
        nc.sync.dma_start(out=w_raw[:].bitcast(I32), in_=w_words[0].bitcast(I32))
        nc.sync.dma_start(out=xo_w[:], in_=words_of(xo_words))

        xt_gs = tile("xt_gs", [P, J], U8)
        xo_gs = tile("xo_gs", [P, J], U8)
        plane1 = tile("plane1", [P, 2 * J + 2 * R], U8)
        nc.vector.tensor_copy(xt_gs[:], xt_s[:].indirect(idx1[:]))
        nc.vector.tensor_copy(xo_gs[:], xo_s[:].indirect(idx2[:]))
        nc.vector.tensor_copy(
            out=plane1[:, 2 * J :].rearrange("p (u t m) -> p u t m", u=2, t=PACK),
            in_=ww_s[:].rearrange("p (u m t) -> p u t m", u=2, t=PACK),
        )
        nc.vector.tensor_copy(out=plane1[:, 0:J].bitcast(I32), in_=xt_gs[:].bitcast(I32))
        nc.vector.tensor_copy(out=plane1[:, J : 2 * J].bitcast(I32), in_=xo_gs[:].bitcast(I32))
        spread(plane1, P - ROWS, (nc.scalar, nc.sync))
        nc.sync.dma_start(idx4[:], offs4)
        nc.sync.dma_start(idx3[:], offs3)

        xt_g = tile("xt_g", [P, J], U32)
        xo_g = tile("xo_g", [P, J], U32)
        w_p = tile("w_p", [P, 2 * R], U8)
        w2_p = tile("w2_p", [P, R], U32)
        nc.vector.tensor_copy(xt_g[:], xt_w[:].bitcast(U32).indirect(idx1[:]))
        nc.vector.tensor_copy(xo_g[:], xo_w[:].bitcast(U32).indirect(idx2[:]))
        nc.scalar.copy(
            out=w_p[:].bitcast(U16).rearrange("p (t m) -> p t m", t=PACK),
            in_=w_raw[:].bitcast(U16).rearrange("p (m t) -> p t m", t=PACK),
        )
        nc.scalar.copy(
            out=w2_p[:].rearrange("p (t m) -> p t m", t=PACK),
            in_=w2_raw[:].bitcast(U32).rearrange("p (m t) -> p t m", t=PACK),
        )

        late = tile("late", [P, 2 * N + J + 4 * N + 4 * J], U8, tag="xt_w")
        plane2 = late[:, 0 : 2 * N + J]
        nc.sync.dma_start(out=plane2[0:ROWS, 0:N].bitcast(I32), in_=wb_scales[0].bitcast(I32))
        nc.sync.dma_start(out=plane2[0:ROWS, N : 2 * N].bitcast(I32), in_=ws_scales[0].bitcast(I32))
        nc.sync.dma_start(out=plane2[0:ROWS, 2 * N : 2 * N + J].bitcast(I32), in_=sx_scales[0].bitcast(I32))
        late_w = late[:, 2 * N + J :]
        wb_w = late_w[:, 0 : 2 * N]
        ws_w = late_w[:, 2 * N : 4 * N]
        sx_w = late_w[:, 4 * N :].bitcast(I32)
        nc.sync.dma_start(out=ws_w.bitcast(I32), in_=ws_words[0].bitcast(I32))
        nc.sync.dma_start(out=wb_w.bitcast(I32), in_=wb_words[0].bitcast(I32))
        nc.sync.dma_start(out=sx_w, in_=words_of(sx_words))
        spread(plane2, 0, (nc.sync,))

        def w_slice(t):
            return w_p[:, 2 * P * t : 2 * P * (t + 1)].bitcast(E2M1), plane1[:, 2 * J + P * t : 2 * J + P * (t + 1)]

        def w2_slice(t):
            return w2_p[:, P * t : P * (t + 1)].bitcast(E5M2), plane1[:, 2 * J + R + P * t : 2 * J + R + P * (t + 1)]

        def xt_slots(c0, c1):
            return xt_g[:, c0:c1].bitcast(E5M2), plane1[:, c0:c1]

        def xo_slots(c0, c1):
            return xo_g[:, c0:c1].bitcast(E4M3), plane1[:, J + c0 : J + c1]

        def wb_block(nb):
            return wb_w[:, 2 * P * nb : 2 * P * (nb + 1)].bitcast(E2M1), plane2[:, P * nb : P * (nb + 1)]

        def ws_block(nb):
            return ws_w[:, 2 * P * nb : 2 * P * (nb + 1)].bitcast(E2M1), plane2[:, N + P * nb : N + P * (nb + 1)]

        def sx_slots(c0, c1):
            return sx_w[:, c0:c1].bitcast(E4M3), plane2[:, 2 * N + c0 : 2 * N + c1]

        a_ps = [ps.tile([P, J], F32, name=f"a_ps{t}", tag=f"bank{t}") for t in range(PACK)]
        a_sb = [tile(f"a_sb{t}", [P, J], F32) for t in range(PACK)]
        for t in range(PACK):
            mx(a_ps[t][:], w_slice(t), xt_slots(0, J), True, False)
            mx(a_ps[t][:], w2_slice(t), xo_slots(0, J), False, True)
        b_ps = [ps.tile([P, PACK, HALF], F32, name=f"b_ps{h}", tag=f"b_bank{h}") for h in range(2)]
        for h in range(2):
            for t in range(PACK):
                mx(b_ps[h][:, t, :], w2_slice(t), xt_slots(h * HALF, (h + 1) * HALF), True, False)
                mx(b_ps[h][:, t, :], w_slice(t), xo_slots(h * HALF, (h + 1) * HALF), False, True)

        diff = [tile(f"diff{h}", [P, PACK, HALF], F32) for h in range(2)]

        def difference(h, t):
            cols = slice(h * HALF // GROUP, (h + 1) * HALF // GROUP)
            other = tile(f"other{h}{t}", [P, HALF], F32)
            nc.scalar.activation(other[:], a_sb[t][:].indirect(idx4[:, cols]), ACT.Copy)
            nc.vector.tensor_tensor(diff[h][:, t, :], a_sb[t][:].indirect(idx3[:, cols]), other[:], ALU.subtract)

        nc.vector.tensor_copy(out=a_sb[0][:], in_=a_ps[0][:])
        nc.vector.tensor_copy(out=a_sb[1][:], in_=a_ps[1][:])
        for t in range(2):
            difference(0, t)
            difference(1, t)
            nc.scalar.copy(out=a_sb[2 + t][:], in_=a_ps[2 + t][:])
        for h in range(2):
            difference(h, 2)
            difference(h, 3)

        for h in range(2):
            c0, c1 = h * HALF, (h + 1) * HALF
            y_ps = []
            for nb in range(2):
                y = ps.tile([P, HALF], F32, name=f"y_ps{h}{nb}", tag=f"bank{2 * h + nb}")
                mx(y[:], ws_block(nb), sx_slots(c0, c1), True, False)
                y_ps.append(y)
            mag = tile(f"mag{h}", [P, 2, HALF, 2], F32)
            for u in range(2):
                nc.scalar.activation(
                    mag[:, u, :, :], diff[h][:, 2 * u : 2 * u + 2, :].rearrange("p e j -> p j e"), ACT.Abs
                )
            hid = tile(f"hid{h}", [P, HALF, 2, 2], BF16)
            nc.vector.tensor_tensor(
                hid[:],
                mag[:].rearrange("p u j e -> p j u e"),
                b_ps[h][:].rearrange("p (u e) j -> p j u e", e=2),
                ALU.max,
            )
            hid_w = tile(f"hid_w{h}", [P, HALF], U32)
            hid_s = tile(f"hid_s{h}", [P, HALF], U8)
            nc.vector.quantize_mx(out=hid_w[:].bitcast(E4M3), scales=hid_s[:], in_=hid[:].rearrange("p j u e -> p (j u e)"))
            for nb in range(2):
                mx(y_ps[nb][:], wb_block(nb), (hid_w[:].bitcast(E4M3), hid_s[:]), False, True)
                res = tile(f"res{h}{nb}", [P, HALF], F32)
                if nb == 0:
                    nc.scalar.copy(out=res[:], in_=y_ps[nb][:])
                    nc.scalar.dma_start(out=out[P * nb : P * (nb + 1), c0:c1], in_=res[:])
                else:
                    nc.vector.tensor_copy(out=res[:], in_=y_ps[nb][:])
                    nc.sync.dma_start(out=out[P * nb : P * (nb + 1), c0:c1], in_=res[:])
